import numpy as np
import ml_dtypes


def mxq(x, axis, fmt="e4m3"):
    dtype, down = {"e4m3": (ml_dtypes.float8_e4m3fn, 7), "e5m2": (ml_dtypes.float8_e5m2, 14)}[fmt]
    v = np.moveaxis(np.asarray(x, np.float32).astype(ml_dtypes.bfloat16).astype(np.float64), axis, -1)
    blocks = v.reshape(v.shape[:-1] + (-1, 32))
    amax = np.abs(blocks).max(-1, keepdims=True)
    byte = np.maximum(np.where(amax > 0, np.frexp(amax)[1] - 1 + 127, 0) - down, 1)
    scale = np.exp2(byte - 127.0)
    codes = (blocks / scale).astype(np.float32).astype(dtype).astype(np.float64)
    return np.moveaxis((codes * scale).reshape(v.shape), -1, axis)


WIDE = False


def mx_kscale(k):
    if not WIDE:
        return np.ones(k)
    levels = np.array([10, -10, 5, -5, 0])
    if k % 512:
        return np.exp2(np.random.permutation(np.resize(levels, k // 32))).repeat(32)
    a = np.empty((k // 512, 16))
    for p in range(k // 512):
        a[p, :8] = np.random.permutation(np.resize(levels, 8))
        for g in range(8):
            far = levels[np.abs(levels - a[p, g]) >= 10]
            a[p, g + 8] = far[np.random.randint(len(far))]
    return np.exp2(a.ravel()).repeat(32)


def f64(x):
    return np.asarray(x).astype(np.float64)


def striped(idx):
    return np.tile(idx.reshape(-1, 16).T, (8, 1)).astype(np.uint16)


def unstriped(offs):
    return offs[:16].T.reshape(-1).astype(np.int64)


E2M1 = np.array([0.0, 0.5, 1.0, 1.5, 2.0, 3.0, 4.0, 6.0, -0.0, -0.5, -1.0, -1.5, -2.0, -3.0, -4.0, -6.0])


def pack_weight(w, fmt):
    k, n = w.shape
    w = f64(np.asarray(w, np.float32).astype(ml_dtypes.bfloat16)).reshape(k // 32, 32, n)
    amax = np.abs(w).max(1)
    if fmt == "e4m3":
        byte = np.frexp(amax)[1] - 1 + 127 - 7
    else:
        mant, ex = np.frexp(amax / 6.0)
        byte = np.where(mant > 0.5, ex, ex - 1) + 127
    byte = np.clip(np.where(amax > 0, byte, 1), 1, 254)
    scaled = (w * np.exp2(127.0 - byte)[:, None, :]).reshape(k, n).astype(np.float32)
    by_word = np.ascontiguousarray(scaled.reshape(k // 512, 128, 4, n).transpose(0, 1, 3, 2))
    if fmt == "e4m3":
        words = by_word.astype(ml_dtypes.float8_e4m3fn).view(np.uint8)
    else:
        c = by_word.astype(ml_dtypes.float4_e2m1fn).view(np.uint8) & 0xF
        words = (c[..., 0::2] | (c[..., 1::2] << 4)).reshape(k // 512, 128, 2 * n)
    return np.ascontiguousarray(words), np.ascontiguousarray(byte.astype(np.uint8).reshape(k // 512, 16, n))


def unpack_weight(words, scales, fmt):
    g, _, n = scales.shape
    words = np.ascontiguousarray(words).reshape(g, 128, n, -1)
    if fmt == "e4m3":
        vals = words.view(ml_dtypes.float8_e4m3fn).astype(np.float64)
    else:
        nib = np.empty((g, 128, n, 4), np.uint8)
        nib[..., 0::2] = words & 0xF
        nib[..., 1::2] = words >> 4
        vals = E2M1[nib]
    vals = vals * np.repeat(np.exp2(scales.astype(np.float64) - 127.0), 8, axis=1)[..., None]
    return vals.transpose(0, 1, 3, 2).reshape(g * 512, n)


def gelu(v):
    return 0.5 * v * (1.0 + np.tanh(np.sqrt(2.0 / np.pi) * (v + 0.044715 * v**3)))


K, T, E, C, H, N = 1024, 512, 12, 128, 512, 128
TOP = 3


def by_expert(wq, xq):
    return np.concatenate([wq[e].T @ xq[:, e * C:(e + 1) * C] for e in range(E)], axis=1)


def setup_inputs():
    n = np.random.standard_normal
    s = mx_kscale(K)[:, None]
    u = mx_kscale(H)
    deal = np.repeat(np.arange(E), C).reshape(TOP, T)[:, np.random.permutation(T)]
    deal = np.take_along_axis(deal, np.argsort(np.random.rand(TOP, T), axis=0), axis=0)
    for _ in range(8):
        s_, t_ = np.random.permutation(T).reshape(2, -1); r = np.random.randint(TOP, size=T // 2); x, y = deal[r, s_].copy(), deal[r, t_].copy()
        ok = ~((deal[:, s_] == y).any(0) | (deal[:, t_] == x).any(0)); deal[r[ok], s_[ok]] = y[ok]; deal[r[ok], t_[ok]] = x[ok]
    order = np.lexsort((np.random.rand(TOP * T), deal.reshape(-1)))
    slot_token = order % T; pos = np.empty(TOP * T, np.int64); pos[order] = np.arange(TOP * T); pos = pos.reshape(TOP, T)
    g = np.random.uniform(0.5, 1.5, (TOP, T)); g = g / g.sum(0)
    x = pack_weight(n((K, T)) * s, "e4m3")
    return {
        "x_words": x[0],
        "x_scales": x[1],
        "w1": (n((E + 1, K, H)) / np.sqrt(K) / s[None] * u[None, None, :]).astype(np.float32),
        "w2": (n((E + 1, H, N)) / np.sqrt(H) / u[None, :, None]).astype(np.float32),
        "gate": np.stack([np.tile(r, (N, 1)) for r in g]).astype(np.float32),
        "offs": striped(slot_token),
        "pos1": striped(pos[0]),
        "pos2": striped(pos[1]),
        "pos3": striped(pos[2]),
    }


def reference(x_words, x_scales, w1, w2, gate, offs, pos1, pos2, pos3):
    idx = unstriped(offs)
    w1q, w2q = mxq(f64(w1), 1, "e4m3"), mxq(f64(w2), 1, "e4m3")
    xs = unpack_weight(x_words, x_scales, "e4m3")
    hs = gelu(w1q[E].T @ xs)
    ys = w2q[E].T @ mxq(hs, 0, "e4m3")
    xq = unpack_weight(x_words, x_scales, "e4m3")[:, idx]
    h = gelu(by_expert(w1q, xq))
    y = by_expert(w2q, mxq(h, 0, "e4m3"))
    return ys + sum(f64(gate[r]) * y[:, unstriped(p)] for r, p in enumerate((pos1, pos2, pos3)))

@@ -1,0 +1,253 @@
+from contextlib import ExitStack
+
+import concourse.mybir as mybir
+from concourse.masks import make_identity
+
+K, T, E, C, H, N = 1024, 512, 12, 128, 512, 128
+TOP = 3
+S = E * C
+FLOPS = 2 * (S + T) * (K * H + H * N)
+
+F32 = mybir.dt.float32
+BF16 = mybir.dt.bfloat16
+I32 = mybir.dt.int32
+U32 = mybir.dt.uint32
+U16 = mybir.dt.uint16
+U8 = mybir.dt.uint8
+FP8X4 = mybir.dt.float8_e4m3fn_x4
+GELU = mybir.ActivationFunctionType.Gelu_apprx_tanh
+MULT = mybir.AluOpType.mult
+ADD = mybir.AluOpType.add
+
+P = 128
+PACK = 4
+K_PASS = P * PACK
+PASSES = K // K_PASS
+PER_COLUMN = 16
+GATHER = 256
+RING = 18
+AHEAD = 15
+LATE_W2 = 6
+HALF = T // 2
+
+
+def tile_moe_shr_mlp_gelu_kernel(
+    tc, x_words, x_scales, w1, w2, gate, offs, pos1, pos2, pos3, out
+):
+    nc = tc.nc
+    with ExitStack() as ctx:
+        keep = ctx.enter_context(tc.tile_pool(name="keep", bufs=1))
+        ring = ctx.enter_context(tc.tile_pool(name="ring", bufs=RING))
+        work = ctx.enter_context(tc.tile_pool(name="work", bufs=4))
+        psum = ctx.enter_context(tc.psum_pool(name="psum", bufs=1))
+
+        x_plane = keep.tile([P, T], U8, align_bytes=64)
+        nc.vector.memset(x_plane[:].bitcast(I32), 0)
+        x_codes = keep.tile([P, PASSES, T], I32, align_bytes=64)
+        nc.sync.dma_start(out=x_codes[:], in_=x_words.rearrange("o p t r -> p o (t r)").bitcast(I32))
+        slot_list = keep.tile([P, S // PER_COLUMN], U16)
+        nc.sync.dma_start(slot_list[:], offs)
+        x_rows = keep.tile([P, T // 4], I32)
+        for q in range(4):
+            rows = slice(32 * q, 32 * q + 4 * PASSES)
+            nc.sync.dma_start(out=x_rows[rows, :], in_=x_scales[:, 4 * q : 4 * q + 4, :].bitcast(I32))
+            nc.vector.tensor_copy(out=x_plane[rows, :].bitcast(I32), in_=x_rows[rows, :])
+        identity = keep.tile([P, P], F32)
+        make_identity(nc, identity[:])
+
+        stream = []
+        for e in [E] + list(range(E)):
+            stream.extend([("w1", e, o) for o in range(PASSES)])
+            if e < E - LATE_W2:
+                stream.append(("w2", e, 0))
+        stream.extend([("w2", e, 0) for e in range(E - LATE_W2, E)])
+        stream.extend([("gate", 0, 0), ("w2", E, 0), ("gate", 1, 0), ("gate", 2, 0)])
+
+        raw = {}
+        grouped = {}
+        quantised = {}
+        hidden = {}
+        gathered = {}
+
+        def load(item):
+            kind, e, o = item
+            if kind == "w1":
+                tile = ring.tile([P, PACK, H], F32, name="w1_raw", tag="ring")
+                src = w1[e, o * K_PASS : (o + 1) * K_PASS, :].rearrange("(p j) c -> p j c", j=PACK)
+            elif kind == "w2":
+                tile = ring.tile([P, PACK, N], F32, name="w2_raw", tag="ring")
+                src = w2[e].rearrange("(p j) c -> p j c", j=PACK)
+            else:
+                tile = ring.tile([P, T], F32, name="gate_row", tag="ring")
+                src = gate[e]
+            nc.sync.dma_start(out=tile[:], in_=src)
+            raw[item] = tile
+
+        def cast(item):
+            kind, e, o = item
+            width = H if kind == "w1" else N
+            tile = work.tile([P, width * PACK], BF16, name=kind + "_grouped", align_bytes=64)
+            dst = tile[:].rearrange("p (c i j) -> p c j i", i=4, j=PACK)
+            src = raw[item][:].rearrange("p j (c i) -> p c j i", i=4)
+            on_scalar = (kind == "w1" and o == 0) or (kind == "w2" and e != E - 1)
+            if on_scalar:
+                nc.scalar.copy(out=dst, in_=src)
+            else:
+                nc.vector.tensor_copy(out=dst, in_=src)
+            grouped[item] = tile
+
+        def quantise(item):
+            kind, e, o = item
+            width = H if kind == "w1" else N
+            codes = work.tile([P, width], U32, name=kind + "_codes", align_bytes=64)
+            plane = work.tile([P, width], U8, name=kind + "_plane", align_bytes=64)
+            nc.vector.quantize_mx(out=codes[:].bitcast(FP8X4), scales=plane[:], in_=grouped[item][:])
+            quantised[item] = (codes, plane)
+
+        def gather(piece):
+            offsets = slot_list[:, piece * GATHER // PER_COLUMN : (piece + 1) * GATHER // PER_COLUMN]
+            words = []
+            for o in range(PASSES):
+                tile = work.tile([P, GATHER], U32, name="slot_codes_%d" % o, bufs=2, align_bytes=64)
+                nc.vector.tensor_copy(tile[:], x_codes[:, o, :].bitcast(U32).indirect(offsets))
+                words.append(tile)
+            plane = work.tile([P, GATHER], U8, name="slot_plane", bufs=2, align_bytes=64)
+            nc.vector.tensor_copy(plane[:], x_plane[:].indirect(offsets))
+            gathered[piece] = (words, plane)
+
+        def block_operands(e, b, o):
+            if e == E:
+                cols = slice(b * C, (b + 1) * C)
+                return x_codes[:, o, cols], x_plane[4 * o : P, cols]
+            piece, first = divmod(e * C, GATHER)
+            words, plane = gathered[piece]
+            return words[o][:, first : first + C], plane[4 * o : P, first : first + C]
+
+        def blocks_of(e):
+            return range(T // C) if e == E else range(1)
+
+        activated = {}
+        turned = {}
+
+        def first_layer(e):
+            for b in blocks_of(e):
+                pre = psum.tile([P, H], F32, name="pre", bufs=3)
+                for o in range(PASSES):
+                    words, plane = block_operands(e, b, o)
+                    codes, scales = quantised[("w1", e, o)]
+                    nc.tensor.matmul_mx(
+                        out=pre[:],
+                        lhsT=words.bitcast(FP8X4),
+                        lhsT_scale=plane,
+                        rhs=codes[:].bitcast(FP8X4),
+                        rhs_scale=scales[:],
+                        start=(o == 0),
+                        stop=(o == PASSES - 1),
+                    )
+                act = work.tile([P, H], BF16, name="act", bufs=6)
+                nc.scalar.activation(
+                    out=act[:].rearrange("s (u p v) -> s u p v", u=2, v=2),
+                    in_=pre[:].rearrange("s (p u v) -> s u p v", u=2, v=2),
+                    func=GELU,
+                )
+                activated[(e, b)] = act
+
+        def turn(e):
+            width = C * len(blocks_of(e))
+            if e == E:
+                pairs = keep.tile([P, width, 2], F32, name="shared_pairs", align_bytes=64)
+            else:
+                pairs = work.tile([P, width, 2], F32, name="pairs", align_bytes=64)
+            for b in blocks_of(e):
+                bank = psum.tile([P, 2, C], F32, name="turn", bufs=2)
+                words = activated[(e, b)][:].bitcast(F32)
+                for u in range(2):
+                    nc.tensor.transpose(bank[:, u, :], words[:, u * P : (u + 1) * P], identity[:])
+                nc.scalar.copy(out=pairs[:, b * C : (b + 1) * C, :], in_=bank[:].rearrange("p u s -> p s u"))
+            turned[e] = pairs
+
+        def quantise_hidden(e):
+            width = C * len(blocks_of(e))
+            if e == E:
+                codes = keep.tile([P, width], U32, name="shared_h_codes", align_bytes=64)
+                plane = keep.tile([P, width], U8, name="shared_h_plane", align_bytes=64)
+            else:
+                codes = work.tile([P, width], U32, name="h_codes", bufs=LATE_W2 + 2, align_bytes=64)
+                plane = work.tile([P, width], U8, name="h_plane", bufs=LATE_W2 + 2, align_bytes=64)
+            values = turned[e][:].rearrange("p s u -> p (s u)").bitcast(BF16)
+            nc.vector.quantize_mx(out=codes[:].bitcast(FP8X4), scales=plane[:], in_=values)
+            hidden[e] = (codes, plane)
+
+        y_slots = keep.tile([P, S], F32)
+        y_shared = psum.tile([P, T], F32)
+
+        def second_layer(e):
+            codes, scales = quantised[("w2", e, 0)]
+            h_codes, h_plane = hidden[e]
+            bank = y_shared if e == E else psum.tile([P, C], F32, name="y_bank", bufs=2)
+            nc.tensor.matmul_mx(
+                out=bank[:],
+                lhsT=codes[:].bitcast(FP8X4),
+                lhsT_scale=scales[:],
+                rhs=h_codes[:].bitcast(FP8X4),
+                rhs_scale=h_plane[:],
+                start=True,
+                stop=True,
+            )
+            if e < E:
+                nc.scalar.copy(out=y_slots[:, e * C : (e + 1) * C], in_=bank[:])
+
+        for item in stream[:3]:
+            load(item)
+        token_lists = []
+        for r, pos in enumerate((pos1, pos2, pos3)):
+            tile = keep.tile([P, T // PER_COLUMN], U16, name="token_list_%d" % r)
+            nc.sync.dma_start(tile[:], pos)
+            token_lists.append(tile)
+        for item in stream[3:AHEAD]:
+            load(item)
+        gather(0)
+
+        done = set()
+        to_quantise, to_turn, to_quantise_hidden = [], [], []
+        for n in range(len(stream) + 4):
+            if n + AHEAD < len(stream):
+                load(stream[n + AHEAD])
+            item = stream[n] if n < len(stream) else None
+            if item is not None and item[0] != "gate":
+                cast(item)
+            for e in to_quantise_hidden:
+                quantise_hidden(e)
+            to_quantise_hidden = to_turn
+            for e in to_turn:
+                turn(e)
+            to_turn = []
+            for ready in to_quantise:
+                quantise(ready)
+                kind, e, o = ready
+                if kind == "w1" and o == PASSES - 1:
+                    first_layer(e)
+                    to_turn.append(e)
+                    nxt = 1 if e == E else e + 2
+                    if nxt < E and nxt * C % GATHER == 0:
+                        gather(nxt * C // GATHER)
+            to_quantise = [item] if item is not None and item[0] != "gate" else []
+            for e in range(E + 1):
+                if e not in done and e in hidden and ("w2", e, 0) in quantised:
+                    second_layer(e)
+                    done.add(e)
+
+        for h in range(2):
+            cols = slice(h * HALF, (h + 1) * HALF)
+            total = y_shared[:, cols]
+            terms = []
+            for r in range(TOP):
+                term = work.tile([P, HALF], F32, name="term", bufs=2 * TOP)
+                offsets = token_lists[r][:, h * HALF // PER_COLUMN : (h + 1) * HALF // PER_COLUMN]
+                nc.vector.tensor_tensor(term[:], y_slots[:].indirect(offsets), raw[("gate", r, 0)][:, cols], MULT)
+                terms.append(term)
+            for r in range(TOP):
+                partial = work.tile([P, HALF], F32, name="partial", bufs=2 * TOP)
+                nc.vector.tensor_tensor(partial[:], terms[r][:], total, ADD)
+                total = partial[:]
+            nc.sync.dma_start(out=out[:, cols], in_=total)

@@ -26,8 +26,12 @@ PASSES = K // K_PASS
 PER_COLUMN = 16
 GATHER = 256
 RING = 18
-AHEAD = 15
-LATE_W2 = 6
+AHEAD = 13
+W2_GROUPS = ((0, 4), (4, 4), (8, 2), (10, 1), (11, 1))
+W2_ON_VECTOR = (4, 10, 11, 12)
+EARLY_AFTER = 5
+VECTOR_SHARE = 108
+LAST_SHARE = 80
 HALF = T // 2
 
 
@@ -58,10 +62,10 @@ def tile_moe_shr_mlp_gelu_kernel(
         stream = []
         for e in [E] + list(range(E)):
             stream.extend([("w1", e, o) for o in range(PASSES)])
-            if e < E - LATE_W2:
-                stream.append(("w2", e, 0))
-        stream.extend([("w2", e, 0) for e in range(E - LATE_W2, E)])
-        stream.extend([("gate", 0, 0), ("w2", E, 0), ("gate", 1, 0), ("gate", 2, 0)])
+            if e == EARLY_AFTER:
+                stream.append(("w2",) + W2_GROUPS[0])
+        stream.extend([("w2",) + group for group in W2_GROUPS[1:]])
+        stream.extend([("gate", 0, 0), ("w2", E, 1), ("gate", 1, 0), ("gate", 2, 0)])
 
         raw = {}
         grouped = {}
@@ -72,36 +76,46 @@ def tile_moe_shr_mlp_gelu_kernel(
         def load(item):
             kind, e, o = item
             if kind == "w1":
-                tile = ring.tile([P, PACK, H], F32, name="w1_raw", tag="ring")
+                tile = ring.tile([P, PACK, H], F32, name="w1_raw", tag="ring", align_bytes=64)
                 src = w1[e, o * K_PASS : (o + 1) * K_PASS, :].rearrange("(p j) c -> p j c", j=PACK)
             elif kind == "w2":
-                tile = ring.tile([P, PACK, N], F32, name="w2_raw", tag="ring")
-                src = w2[e].rearrange("(p j) c -> p j c", j=PACK)
+                tile = ring.tile([P, o, PACK * N], F32, name="w2_raw", tag="ring", align_bytes=64)
+                src = w2[e : e + o].rearrange("g (p j) c -> p g (j c)", j=PACK)
             else:
-                tile = ring.tile([P, T], F32, name="gate_row", tag="ring")
+                tile = ring.tile([P, T], F32, name="gate_row", tag="ring", align_bytes=64)
                 src = gate[e]
             nc.sync.dma_start(out=tile[:], in_=src)
             raw[item] = tile
 
         def cast(item):
             kind, e, o = item
-            width = H if kind == "w1" else N
-            tile = work.tile([P, width * PACK], BF16, name=kind + "_grouped", align_bytes=64)
-            dst = tile[:].rearrange("p (c i j) -> p c j i", i=4, j=PACK)
-            src = raw[item][:].rearrange("p j (c i) -> p c j i", i=4)
-            on_scalar = (kind == "w1" and o == 0) or (kind == "w2" and e != E - 1)
-            if on_scalar:
-                nc.scalar.copy(out=dst, in_=src)
+            tile = work.tile([P, H * PACK], BF16, name="grouped", align_bytes=64)
+            if kind == "w1":
+                dst = tile[:].rearrange("p (c i j) -> p c j i", i=4, j=PACK)
+                src = raw[item][:].rearrange("p j (c i) -> p c j i", i=4)
+                cut = 0 if o == 0 else (LAST_SHARE if e == E - 1 else VECTOR_SHARE)
+                if cut > 0:
+                    nc.vector.tensor_copy(out=dst[:, :cut], in_=src[:, :cut])
+                nc.scalar.copy(out=dst[:, cut:], in_=src[:, cut:])
+                grouped[item] = tile[:]
             else:
-                nc.vector.tensor_copy(out=dst, in_=src)
-            grouped[item] = tile
+                used = tile[:, 0 : o * N * PACK]
+                dst = used.rearrange("p (g c i j) -> p g c j i", g=o, i=4, j=PACK)
+                src = raw[item][:].rearrange("p g (j c i) -> p g c j i", i=4, j=PACK)
+                if o == 1:
+                    dst, src = dst[:, 0], src[:, 0]
+                if e in W2_ON_VECTOR:
+                    nc.vector.tensor_copy(out=dst, in_=src)
+                else:
+                    nc.scalar.copy(out=dst, in_=src)
+                grouped[item] = used
 
         def quantise(item):
             kind, e, o = item
-            width = H if kind == "w1" else N
-            codes = work.tile([P, width], U32, name=kind + "_codes", align_bytes=64)
-            plane = work.tile([P, width], U8, name=kind + "_plane", align_bytes=64)
-            nc.vector.quantize_mx(out=codes[:].bitcast(FP8X4), scales=plane[:], in_=grouped[item][:])
+            width = H if kind == "w1" else o * N
+            codes = work.tile([P, H], U32, name="codes", bufs=6, align_bytes=64)
+            plane = work.tile([P, H], U8, name="plane", bufs=6, align_bytes=64)
+            nc.vector.quantize_mx(out=codes[:, 0:width].bitcast(FP8X4), scales=plane[:, 0:width], in_=grouped[item])
             quantised[item] = (codes, plane)
 
         def gather(piece):
@@ -127,11 +141,18 @@ def tile_moe_shr_mlp_gelu_kernel(
             return range(T // C) if e == E else range(1)
 
         activated = {}
+        summed = {}
+        banks = {}
         turned = {}
+        order = [E] + list(range(E))
+
+        def spent(e, steps):
+            later = order.index(e) + steps
+            return raw[("w1", order[later], 0)] if later < len(order) else None
 
         def first_layer(e):
             for b in blocks_of(e):
-                pre = psum.tile([P, H], F32, name="pre", bufs=3)
+                pre = psum.tile([P, H], F32, name="pre", tag="sums", bufs=5)
                 for o in range(PASSES):
                     words, plane = block_operands(e, b, o)
                     codes, scales = quantised[("w1", e, o)]
@@ -144,26 +165,43 @@ def tile_moe_shr_mlp_gelu_kernel(
                         start=(o == 0),
                         stop=(o == PASSES - 1),
                     )
-                act = work.tile([P, H], BF16, name="act", bufs=6)
+                summed[(e, b)] = pre
+
+        def activate(e):
+            room = spent(e, 1)
+            if room is None:
+                room = keep.tile([P, 1, H // 2], F32, name="last_act")
+            for b in blocks_of(e):
+                act = room[:, b, 0 : H // 2]
                 nc.scalar.activation(
-                    out=act[:].rearrange("s (u p v) -> s u p v", u=2, v=2),
-                    in_=pre[:].rearrange("s (p u v) -> s u p v", u=2, v=2),
+                    out=act.bitcast(BF16).rearrange("s (u p v) -> s u p v", u=2, v=2),
+                    in_=summed[(e, b)][:].rearrange("s (p u v) -> s u p v", u=2, v=2),
                     func=GELU,
                 )
                 activated[(e, b)] = act
 
         def turn(e):
-            width = C * len(blocks_of(e))
-            if e == E:
-                pairs = keep.tile([P, width, 2], F32, name="shared_pairs", align_bytes=64)
+            blocks = blocks_of(e)
+            for first in range(0, len(blocks), 2):
+                bank = psum.tile([P, 2, 2, C], F32, name="turn", bufs=2)
+                for b in blocks[first : first + 2]:
+                    for u in range(2):
+                        nc.tensor.transpose(
+                            bank[:, b - first, u, :], activated[(e, b)][:, u * P : (u + 1) * P], identity[:]
+                        )
+                banks[(e, first)] = bank
+
+        def weave(e):
+            blocks = blocks_of(e)
+            room = spent(e, 2)
+            if room is None:
+                pairs = work.tile([P, 2 * C], F32, name="last_pairs", bufs=2, align_bytes=64)[:]
             else:
-                pairs = work.tile([P, width, 2], F32, name="pairs", align_bytes=64)
-            for b in blocks_of(e):
-                bank = psum.tile([P, 2, C], F32, name="turn", bufs=2)
-                words = activated[(e, b)][:].bitcast(F32)
-                for u in range(2):
-                    nc.tensor.transpose(bank[:, u, :], words[:, u * P : (u + 1) * P], identity[:])
-                nc.scalar.copy(out=pairs[:, b * C : (b + 1) * C, :], in_=bank[:].rearrange("p u s -> p s u"))
+                pairs = room[:].rearrange("p j c -> p (j c)")[:, 2 * H : 2 * H + 2 * C * len(blocks)]
+            for first in range(0, len(blocks), 2):
+                count = len(blocks[first : first + 2])
+                dst = pairs[:, 2 * C * first : 2 * C * (first + count)].rearrange("p (b s u) -> p b s u", b=count, u=2)
+                nc.scalar.copy(out=dst, in_=banks[(e, first)][:, 0:count].rearrange("p b u s -> p b s u"))
             turned[e] = pairs
 
         def quantise_hidden(e):
@@ -172,30 +210,33 @@ def tile_moe_shr_mlp_gelu_kernel(
                 codes = keep.tile([P, width], U32, name="shared_h_codes", align_bytes=64)
                 plane = keep.tile([P, width], U8, name="shared_h_plane", align_bytes=64)
             else:
-                codes = work.tile([P, width], U32, name="h_codes", bufs=LATE_W2 + 2, align_bytes=64)
-                plane = work.tile([P, width], U8, name="h_plane", bufs=LATE_W2 + 2, align_bytes=64)
-            values = turned[e][:].rearrange("p s u -> p (s u)").bitcast(BF16)
+                codes = work.tile([P, width], U32, name="h_codes", bufs=E, align_bytes=64)
+                plane = work.tile([P, width], U8, name="h_plane", bufs=E, align_bytes=64)
+            values = turned[e].bitcast(BF16)
             nc.vector.quantize_mx(out=codes[:].bitcast(FP8X4), scales=plane[:], in_=values)
             hidden[e] = (codes, plane)
 
         y_slots = keep.tile([P, S], F32)
         y_shared = psum.tile([P, T], F32)
 
-        def second_layer(e):
-            codes, scales = quantised[("w2", e, 0)]
-            h_codes, h_plane = hidden[e]
-            bank = y_shared if e == E else psum.tile([P, C], F32, name="y_bank", bufs=2)
-            nc.tensor.matmul_mx(
-                out=bank[:],
-                lhsT=codes[:].bitcast(FP8X4),
-                lhsT_scale=scales[:],
-                rhs=h_codes[:].bitcast(FP8X4),
-                rhs_scale=h_plane[:],
-                start=True,
-                stop=True,
-            )
-            if e < E:
-                nc.scalar.copy(out=y_slots[:, e * C : (e + 1) * C], in_=bank[:])
+        def second_layer(item):
+            kind, first, count = item
+            codes, scales = quantised[item]
+            bank = y_shared if first == E else psum.tile([P, H], F32, name="y_bank", tag="sums", bufs=5)
+            for g in range(count):
+                h_codes, h_plane = hidden[first + g]
+                cols = slice(g * N, (g + 1) * N)
+                nc.tensor.matmul_mx(
+                    out=bank[:] if first == E else bank[:, g * C : (g + 1) * C],
+                    lhsT=codes[:, cols].bitcast(FP8X4),
+                    lhsT_scale=scales[:, cols],
+                    rhs=h_codes[:].bitcast(FP8X4),
+                    rhs_scale=h_plane[:],
+                    start=True,
+                    stop=True,
+                )
+            if first < E:
+                nc.scalar.copy(out=y_slots[:, first * C : (first + count) * C], in_=bank[:, 0 : count * C])
 
         for item in stream[:3]:
             load(item)
@@ -209,33 +250,48 @@ def tile_moe_shr_mlp_gelu_kernel(
         gather(0)
 
         done = set()
-        to_quantise, to_turn, to_quantise_hidden = [], [], []
+        cast_done = set()
+        to_quantise = []
+
+        def advance():
+            for e in order:
+                for stage, needs, steps in (
+                    (quantise_hidden, weave, 0),
+                    (weave, turn, 2),
+                    (turn, activate, 0),
+                    (activate, first_layer, 1),
+                ):
+                    later = order.index(e) + steps
+                    free = later >= len(order) or ("w1", order[later], 0) in cast_done
+                    if (stage, e) not in done and (needs, e) in done and free:
+                        stage(e)
+                        done.add((stage, e))
+                        break
+            for item in stream:
+                kind, first, count = item
+                if kind == "w2" and item in quantised and item not in done:
+                    if all(first + g in hidden for g in range(count)):
+                        second_layer(item)
+                        done.add(item)
+
         for n in range(len(stream) + 4):
             if n + AHEAD < len(stream):
                 load(stream[n + AHEAD])
             item = stream[n] if n < len(stream) else None
             if item is not None and item[0] != "gate":
                 cast(item)
-            for e in to_quantise_hidden:
-                quantise_hidden(e)
-            to_quantise_hidden = to_turn
-            for e in to_turn:
-                turn(e)
-            to_turn = []
+                cast_done.add(item)
+            advance()
             for ready in to_quantise:
                 quantise(ready)
                 kind, e, o = ready
                 if kind == "w1" and o == PASSES - 1:
                     first_layer(e)
-                    to_turn.append(e)
+                    done.add((first_layer, e))
                     nxt = 1 if e == E else e + 2
                     if nxt < E and nxt * C % GATHER == 0:
                         gather(nxt * C // GATHER)
             to_quantise = [item] if item is not None and item[0] != "gate" else []
-            for e in range(E + 1):
-                if e not in done and e in hidden and ("w2", e, 0) in quantised:
-                    second_layer(e)
-                    done.add(e)
 
         for h in range(2):
             cols = slice(h * HALF, (h + 1) * HALF)

@@ -6,6 +6,7 @@ from concourse.masks import make_identity
 K, T, E, C, H, N = 1024, 512, 12, 128, 512, 128
 TOP = 3
 S = E * C
+SHARED = E
 FLOPS = 2 * (S + T) * (K * H + H * N)
 
 F32 = mybir.dt.float32
@@ -23,15 +24,19 @@ P = 128
 PACK = 4
 K_PASS = P * PACK
 PASSES = K // K_PASS
+QUADRANT = 32
+SCALE_ROWS = 4
 PER_COLUMN = 16
-GATHER = 256
-RING = 18
-AHEAD = 13
-W2_GROUPS = ((0, 4), (4, 4), (8, 2), (10, 1), (11, 1))
-W2_ON_VECTOR = (4, 10, 11, 12)
-EARLY_AFTER = 5
-VECTOR_SHARE = 108
-LAST_SHARE = 80
+RUN = 4
+RUNS = H // RUN
+GATHER = 384
+W1_SLOTS = 7
+AHEAD = 4
+ORDER = (SHARED,) + tuple(range(E))
+BY_PASS = (ORDER[0], ORDER[-2], ORDER[-1])
+VECTOR_RUNS = 72
+W2_LOADS = tuple((e, 2) for e in range(0, E - 2, 2)) + ((E - 2, 1), (E - 1, 1), (SHARED, 1))
+SUM_BANKS = 5
 HALF = T // 2
 
 
@@ -41,7 +46,7 @@ def tile_moe_shr_mlp_gelu_kernel(
     nc = tc.nc
     with ExitStack() as ctx:
         keep = ctx.enter_context(tc.tile_pool(name="keep", bufs=1))
-        ring = ctx.enter_context(tc.tile_pool(name="ring", bufs=RING))
+        ring = ctx.enter_context(tc.tile_pool(name="ring", bufs=W1_SLOTS))
         work = ctx.enter_context(tc.tile_pool(name="work", bufs=4))
         psum = ctx.enter_context(tc.psum_pool(name="psum", bufs=1))
 
@@ -52,255 +57,234 @@ def tile_moe_shr_mlp_gelu_kernel(
         slot_list = keep.tile([P, S // PER_COLUMN], U16)
         nc.sync.dma_start(slot_list[:], offs)
         x_rows = keep.tile([P, T // 4], I32)
-        for q in range(4):
-            rows = slice(32 * q, 32 * q + 4 * PASSES)
-            nc.sync.dma_start(out=x_rows[rows, :], in_=x_scales[:, 4 * q : 4 * q + 4, :].bitcast(I32))
+        for q in range(P // QUADRANT):
+            rows = slice(QUADRANT * q, QUADRANT * q + SCALE_ROWS * PASSES)
+            blocks = slice(SCALE_ROWS * q, SCALE_ROWS * (q + 1))
+            nc.scalar.dma_start(out=x_rows[rows, :], in_=x_scales[:, blocks, :].bitcast(I32))
             nc.vector.tensor_copy(out=x_plane[rows, :].bitcast(I32), in_=x_rows[rows, :])
+
+        warm = keep.tile([P, 2], F32)
+        nc.vector.memset(warm[:, 0:1], 0.0)
+        nc.scalar.activation(out=warm[:, 1:2], in_=warm[:, 0:1], func=GELU)
+
         identity = keep.tile([P, P], F32)
         make_identity(nc, identity[:])
 
-        stream = []
-        for e in [E] + list(range(E)):
-            stream.extend([("w1", e, o) for o in range(PASSES)])
-            if e == EARLY_AFTER:
-                stream.append(("w2",) + W2_GROUPS[0])
-        stream.extend([("w2",) + group for group in W2_GROUPS[1:]])
-        stream.extend([("gate", 0, 0), ("w2", E, 1), ("gate", 1, 0), ("gate", 2, 0)])
+        w1_raw, w1_rounded, w1_mx = {}, {}, {}
+        w2_raw, w2_rounded, w2_mx = {}, {}, {}
+        slot_mx, sums, pairs, turned, woven, h_mx = {}, {}, {}, {}, {}, {}
 
-        raw = {}
-        grouped = {}
-        quantised = {}
-        hidden = {}
-        gathered = {}
+        def batches(e):
+            return range(T // C if e == SHARED else 1)
 
-        def load(item):
-            kind, e, o = item
-            if kind == "w1":
-                tile = ring.tile([P, PACK, H], F32, name="w1_raw", tag="ring", align_bytes=64)
-                src = w1[e, o * K_PASS : (o + 1) * K_PASS, :].rearrange("(p j) c -> p j c", j=PACK)
-            elif kind == "w2":
-                tile = ring.tile([P, o, PACK * N], F32, name="w2_raw", tag="ring", align_bytes=64)
-                src = w2[e : e + o].rearrange("g (p j) c -> p g (j c)", j=PACK)
+        def load_w1(e):
+            for first, count in ((0, 1), (1, 1)) if e in BY_PASS else ((0, PASSES),):
+                tile = ring.tile([P, count, PACK * H], F32, name="w1_tile", align_bytes=64)
+                rows = w1[e, first * K_PASS : (first + count) * K_PASS, :]
+                nc.sync.dma_start(out=tile[:], in_=rows.rearrange("(o p j) c -> p o (j c)", p=P, j=PACK))
+                for o in range(count):
+                    w1_raw[(e, first + o)] = tile[:, o, :]
+
+        def load_w2(first, count):
+            tile = keep.tile([P, count, PACK * N], F32, name="w2_tile_%d" % first)
+            nc.sync.dma_start(out=tile[:], in_=w2[first : first + count].rearrange("g (p j) n -> p g (j n)", j=PACK))
+            w2_raw[first] = tile
+
+        def round_w1(e, o):
+            tile = work.tile([P, H * PACK], BF16, name="rounded", align_bytes=64)
+            dst = tile[:].rearrange("p (c i j) -> p c j i", i=RUN, j=PACK)
+            src = w1_raw[(e, o)].rearrange("p (j c i) -> p c j i", i=RUN, j=PACK)
+            if e == SHARED:
+                cut = 0
+            elif e in BY_PASS:
+                cut = VECTOR_RUNS
             else:
-                tile = ring.tile([P, T], F32, name="gate_row", tag="ring", align_bytes=64)
-                src = gate[e]
-            nc.sync.dma_start(out=tile[:], in_=src)
-            raw[item] = tile
-
-        def cast(item):
-            kind, e, o = item
-            tile = work.tile([P, H * PACK], BF16, name="grouped", align_bytes=64)
-            if kind == "w1":
-                dst = tile[:].rearrange("p (c i j) -> p c j i", i=4, j=PACK)
-                src = raw[item][:].rearrange("p j (c i) -> p c j i", i=4)
-                cut = 0 if o == 0 else (LAST_SHARE if e == E - 1 else VECTOR_SHARE)
-                if cut > 0:
-                    nc.vector.tensor_copy(out=dst[:, :cut], in_=src[:, :cut])
+                cut = RUNS if o == 0 else 0
+            if cut > 0:
+                nc.vector.tensor_copy(out=dst[:, :cut], in_=src[:, :cut])
+            if cut < RUNS:
                 nc.scalar.copy(out=dst[:, cut:], in_=src[:, cut:])
-                grouped[item] = tile[:]
+            w1_rounded[(e, o)] = tile[:]
+
+        def round_w2(first, count, on_vector):
+            tile = work.tile([P, H * PACK], BF16, name="rounded", align_bytes=64)
+            used = tile[:, 0 : count * N * PACK]
+            dst = used.rearrange("p (g c i j) -> p g c j i", g=count, i=RUN, j=PACK)
+            src = w2_raw[first][:].rearrange("p g (j c i) -> p g c j i", i=RUN, j=PACK)
+            if count == 1:
+                dst, src = dst[:, 0], src[:, 0]
+            if on_vector:
+                nc.vector.tensor_copy(out=dst, in_=src)
             else:
-                used = tile[:, 0 : o * N * PACK]
-                dst = used.rearrange("p (g c i j) -> p g c j i", g=o, i=4, j=PACK)
-                src = raw[item][:].rearrange("p g (j c i) -> p g c j i", i=4, j=PACK)
-                if o == 1:
-                    dst, src = dst[:, 0], src[:, 0]
-                if e in W2_ON_VECTOR:
-                    nc.vector.tensor_copy(out=dst, in_=src)
-                else:
-                    nc.scalar.copy(out=dst, in_=src)
-                grouped[item] = used
+                nc.scalar.copy(out=dst, in_=src)
+            w2_rounded[first] = used
 
-        def quantise(item):
-            kind, e, o = item
-            width = H if kind == "w1" else o * N
-            codes = work.tile([P, H], U32, name="codes", bufs=6, align_bytes=64)
-            plane = work.tile([P, H], U8, name="plane", bufs=6, align_bytes=64)
-            nc.vector.quantize_mx(out=codes[:, 0:width].bitcast(FP8X4), scales=plane[:, 0:width], in_=grouped[item])
-            quantised[item] = (codes, plane)
+        def quantise(values, pool, name, bufs):
+            width = values.shape[1] // PACK
+            words = pool.tile([P, width], U32, name=name + "_words", bufs=bufs, align_bytes=64)
+            plane = pool.tile([P, width], U8, name=name + "_plane", bufs=bufs, align_bytes=64)
+            nc.vector.quantize_mx(out=words[:].bitcast(FP8X4), scales=plane[:], in_=values)
+            return words, plane
 
-        def gather(piece):
+        def gather_slots(piece):
             offsets = slot_list[:, piece * GATHER // PER_COLUMN : (piece + 1) * GATHER // PER_COLUMN]
             words = []
             for o in range(PASSES):
-                tile = work.tile([P, GATHER], U32, name="slot_codes_%d" % o, bufs=2, align_bytes=64)
+                tile = keep.tile([P, GATHER], U32, name="slot_words_%d_%d" % (piece, o), align_bytes=64)
                 nc.vector.tensor_copy(tile[:], x_codes[:, o, :].bitcast(U32).indirect(offsets))
                 words.append(tile)
-            plane = work.tile([P, GATHER], U8, name="slot_plane", bufs=2, align_bytes=64)
+            plane = keep.tile([P, GATHER], U8, name="slot_plane_%d" % piece, align_bytes=64)
             nc.vector.tensor_copy(plane[:], x_plane[:].indirect(offsets))
-            gathered[piece] = (words, plane)
+            slot_mx[piece] = (words, plane)
 
-        def block_operands(e, b, o):
-            if e == E:
-                cols = slice(b * C, (b + 1) * C)
-                return x_codes[:, o, cols], x_plane[4 * o : P, cols]
-            piece, first = divmod(e * C, GATHER)
-            words, plane = gathered[piece]
-            return words[o][:, first : first + C], plane[4 * o : P, first : first + C]
-
-        def blocks_of(e):
-            return range(T // C) if e == E else range(1)
-
-        activated = {}
-        summed = {}
-        banks = {}
-        turned = {}
-        order = [E] + list(range(E))
-
-        def spent(e, steps):
-            later = order.index(e) + steps
-            return raw[("w1", order[later], 0)] if later < len(order) else None
-
-        def first_layer(e):
-            for b in blocks_of(e):
-                pre = psum.tile([P, H], F32, name="pre", tag="sums", bufs=5)
+        def first_product(e):
+            for b in batches(e):
+                bank = psum.tile([P, H], F32, name="pre_activation", tag="sums", bufs=SUM_BANKS)
                 for o in range(PASSES):
-                    words, plane = block_operands(e, b, o)
-                    codes, scales = quantised[("w1", e, o)]
+                    if e == SHARED:
+                        cols = slice(b * C, (b + 1) * C)
+                        x_word, x_scale = x_codes[:, o, cols], x_plane[SCALE_ROWS * o : P, cols]
+                    else:
+                        piece, start = divmod(e * C, GATHER)
+                        cols = slice(start, start + C)
+                        x_word, x_scale = slot_mx[piece][0][o][:, cols], slot_mx[piece][1][SCALE_ROWS * o : P, cols]
+                    words, plane = w1_mx[(e, o)]
                     nc.tensor.matmul_mx(
-                        out=pre[:],
-                        lhsT=words.bitcast(FP8X4),
-                        lhsT_scale=plane,
-                        rhs=codes[:].bitcast(FP8X4),
-                        rhs_scale=scales[:],
+                        out=bank[:],
+                        lhsT=x_word.bitcast(FP8X4),
+                        lhsT_scale=x_scale,
+                        rhs=words[:].bitcast(FP8X4),
+                        rhs_scale=plane[:],
                         start=(o == 0),
                         stop=(o == PASSES - 1),
                     )
-                summed[(e, b)] = pre
+                sums[(e, b)] = bank
 
-        def activate(e):
-            room = spent(e, 1)
-            if room is None:
-                room = keep.tile([P, 1, H // 2], F32, name="last_act")
-            for b in blocks_of(e):
-                act = room[:, b, 0 : H // 2]
+        def spent_weights(step):
+            e = ORDER[step]
+            return w1_raw[(e, 0 if e in BY_PASS else 1)]
+
+        def activate(step):
+            e = ORDER[step]
+            if step + 1 < len(ORDER):
+                room = spent_weights(step + 1)
+            else:
+                room = keep.tile([P, H // 2], F32, name="last_pairs")[:]
+            for b in batches(e):
+                pairs[(e, b)] = room[:, b * H // 2 : (b + 1) * H // 2]
                 nc.scalar.activation(
-                    out=act.bitcast(BF16).rearrange("s (u p v) -> s u p v", u=2, v=2),
-                    in_=summed[(e, b)][:].rearrange("s (p u v) -> s u p v", u=2, v=2),
+                    out=pairs[(e, b)].bitcast(BF16).rearrange("s (u p v) -> s u p v", u=2, v=2),
+                    in_=sums[(e, b)][:].rearrange("s (p u v) -> s u p v", u=2, v=2),
                     func=GELU,
                 )
-                activated[(e, b)] = act
 
-        def turn(e):
-            blocks = blocks_of(e)
-            for first in range(0, len(blocks), 2):
-                bank = psum.tile([P, 2, 2, C], F32, name="turn", bufs=2)
-                for b in blocks[first : first + 2]:
+        def turn(step):
+            e = ORDER[step]
+            for first in batches(e)[::2]:
+                bank = psum.tile([P, 2, 2, C], F32, name="turned_pairs", bufs=2)
+                for b in batches(e)[first : first + 2]:
                     for u in range(2):
-                        nc.tensor.transpose(
-                            bank[:, b - first, u, :], activated[(e, b)][:, u * P : (u + 1) * P], identity[:]
-                        )
-                banks[(e, first)] = bank
+                        nc.tensor.transpose(bank[:, b - first, u, :], pairs[(e, b)][:, u * P : (u + 1) * P], identity[:])
+                turned[(e, first)] = bank
 
-        def weave(e):
-            blocks = blocks_of(e)
-            room = spent(e, 2)
-            if room is None:
-                pairs = work.tile([P, 2 * C], F32, name="last_pairs", bufs=2, align_bytes=64)[:]
+        def weave(step):
+            e = ORDER[step]
+            width = 2 * C * len(batches(e))
+            if step + 2 < len(ORDER):
+                room = spent_weights(step + 2)[:, 2 * H : 2 * H + width]
             else:
-                pairs = room[:].rearrange("p j c -> p (j c)")[:, 2 * H : 2 * H + 2 * C * len(blocks)]
-            for first in range(0, len(blocks), 2):
-                count = len(blocks[first : first + 2])
-                dst = pairs[:, 2 * C * first : 2 * C * (first + count)].rearrange("p (b s u) -> p b s u", b=count, u=2)
-                nc.scalar.copy(out=dst, in_=banks[(e, first)][:, 0:count].rearrange("p b u s -> p b s u"))
-            turned[e] = pairs
+                room = work.tile([P, width], F32, name="last_woven", bufs=2, align_bytes=64)[:]
+            for first in batches(e)[::2]:
+                count = len(batches(e)[first : first + 2])
+                dst = room[:, 2 * C * first : 2 * C * (first + count)].rearrange("p (b s u) -> p b s u", b=count, u=2)
+                nc.scalar.copy(out=dst, in_=turned[(e, first)][:, 0:count].rearrange("p b u s -> p b s u"))
+            woven[e] = room
 
-        def quantise_hidden(e):
-            width = C * len(blocks_of(e))
-            if e == E:
-                codes = keep.tile([P, width], U32, name="shared_h_codes", align_bytes=64)
-                plane = keep.tile([P, width], U8, name="shared_h_plane", align_bytes=64)
-            else:
-                codes = work.tile([P, width], U32, name="h_codes", bufs=E, align_bytes=64)
-                plane = work.tile([P, width], U8, name="h_plane", bufs=E, align_bytes=64)
-            values = turned[e].bitcast(BF16)
-            nc.vector.quantize_mx(out=codes[:].bitcast(FP8X4), scales=plane[:], in_=values)
-            hidden[e] = (codes, plane)
+        def quantise_hidden(step):
+            e = ORDER[step]
+            h_mx[e] = quantise(woven[e].bitcast(BF16), keep, "h_%d" % e, 1)
 
         y_slots = keep.tile([P, S], F32)
         y_shared = psum.tile([P, T], F32)
 
-        def second_layer(item):
-            kind, first, count = item
-            codes, scales = quantised[item]
-            bank = y_shared if first == E else psum.tile([P, H], F32, name="y_bank", tag="sums", bufs=5)
+        def second_product(first, count):
+            words, plane = w2_mx[first]
+            if first == SHARED:
+                bank = y_shared
+            else:
+                bank = psum.tile([P, count * C], F32, name="y_bank", tag="sums", bufs=SUM_BANKS)
             for g in range(count):
-                h_codes, h_plane = hidden[first + g]
-                cols = slice(g * N, (g + 1) * N)
+                h_words, h_plane = h_mx[first + g]
+                width = h_words.shape[1]
                 nc.tensor.matmul_mx(
-                    out=bank[:] if first == E else bank[:, g * C : (g + 1) * C],
-                    lhsT=codes[:, cols].bitcast(FP8X4),
-                    lhsT_scale=scales[:, cols],
-                    rhs=h_codes[:].bitcast(FP8X4),
+                    out=bank[:, g * width : (g + 1) * width],
+                    lhsT=words[:, g * N : (g + 1) * N].bitcast(FP8X4),
+                    lhsT_scale=plane[:, g * N : (g + 1) * N],
+                    rhs=h_words[:].bitcast(FP8X4),
                     rhs_scale=h_plane[:],
                     start=True,
                     stop=True,
                 )
-            if first < E:
-                nc.scalar.copy(out=y_slots[:, first * C : (first + count) * C], in_=bank[:, 0 : count * C])
+            if first != SHARED:
+                nc.scalar.copy(out=y_slots[:, first * C : (first + count) * C], in_=bank[:])
 
-        for item in stream[:3]:
-            load(item)
-        token_lists = []
-        for r, pos in enumerate((pos1, pos2, pos3)):
-            tile = keep.tile([P, T // PER_COLUMN], U16, name="token_list_%d" % r)
-            nc.sync.dma_start(tile[:], pos)
-            token_lists.append(tile)
-        for item in stream[3:AHEAD]:
-            load(item)
-        gather(0)
+        gates, token_lists = [], []
 
-        done = set()
-        cast_done = set()
-        to_quantise = []
+        def load_gate(r):
+            tile = keep.tile([P, T], F32, name="gate_%d" % r)
+            nc.sync.dma_start(out=tile[:], in_=gate[r])
+            gates.append(tile)
 
-        def advance():
-            for e in order:
-                for stage, needs, steps in (
-                    (quantise_hidden, weave, 0),
-                    (weave, turn, 2),
-                    (turn, activate, 0),
-                    (activate, first_layer, 1),
-                ):
-                    later = order.index(e) + steps
-                    free = later >= len(order) or ("w1", order[later], 0) in cast_done
-                    if (stage, e) not in done and (needs, e) in done and free:
-                        stage(e)
-                        done.add((stage, e))
-                        break
-            for item in stream:
-                kind, first, count = item
-                if kind == "w2" and item in quantised and item not in done:
-                    if all(first + g in hidden for g in range(count)):
-                        second_layer(item)
-                        done.add(item)
+        def load_rest():
+            for first, count in W2_LOADS[:-1]:
+                load_w2(first, count)
+            load_gate(0)
+            for r, pos in enumerate((pos1, pos2, pos3)):
+                tile = keep.tile([P, T // PER_COLUMN], U16, name="token_list_%d" % r)
+                nc.sync.dma_start(tile[:], pos)
+                token_lists.append(tile)
+            load_w2(*W2_LOADS[-1])
+            for r in range(1, TOP):
+                load_gate(r)
 
-        for n in range(len(stream) + 4):
-            if n + AHEAD < len(stream):
-                load(stream[n + AHEAD])
-            item = stream[n] if n < len(stream) else None
-            if item is not None and item[0] != "gate":
-                cast(item)
-                cast_done.add(item)
-            advance()
-            for ready in to_quantise:
-                quantise(ready)
-                kind, e, o = ready
-                if kind == "w1" and o == PASSES - 1:
-                    first_layer(e)
-                    done.add((first_layer, e))
-                    nxt = 1 if e == E else e + 2
-                    if nxt < E and nxt * C % GATHER == 0:
-                        gather(nxt * C // GATHER)
-            to_quantise = [item] if item is not None and item[0] != "gate" else []
+        for e in ORDER[:AHEAD]:
+            load_w1(e)
+        for piece in range(S // GATHER):
+            gather_slots(piece)
 
-        for h in range(2):
-            cols = slice(h * HALF, (h + 1) * HALF)
+        for step in range(len(ORDER) + 2):
+            if step + AHEAD < len(ORDER):
+                load_w1(ORDER[step + AHEAD])
+            elif step + AHEAD == len(ORDER):
+                load_rest()
+            if step < len(ORDER):
+                for o in range(PASSES):
+                    round_w1(ORDER[step], o)
+            if step >= 2:
+                weave(step - 2)
+            if 1 <= step <= len(ORDER):
+                activate(step - 1)
+                turn(step - 1)
+            if step < len(ORDER):
+                for o in range(PASSES):
+                    w1_mx[(ORDER[step], o)] = quantise(w1_rounded[(ORDER[step], o)], work, "w1", 4)
+                first_product(ORDER[step])
+            if step >= 2:
+                quantise_hidden(step - 2)
+
+        for turn_number, (first, count) in enumerate(W2_LOADS):
+            round_w2(first, count, turn_number % 2 == 0)
+            w2_mx[first] = quantise(w2_rounded[first], work, "w2", 4)
+            second_product(first, count)
+
+        for half in range(2):
+            cols = slice(half * HALF, (half + 1) * HALF)
             total = y_shared[:, cols]
             terms = []
             for r in range(TOP):
                 term = work.tile([P, HALF], F32, name="term", bufs=2 * TOP)
-                offsets = token_lists[r][:, h * HALF // PER_COLUMN : (h + 1) * HALF // PER_COLUMN]
-                nc.vector.tensor_tensor(term[:], y_slots[:].indirect(offsets), raw[("gate", r, 0)][:, cols], MULT)
+                offsets = token_lists[r][:, half * HALF // PER_COLUMN : (half + 1) * HALF // PER_COLUMN]
+                nc.vector.tensor_tensor(term[:], y_slots[:].indirect(offsets), gates[r][:, cols], MULT)
                 terms.append(term)
             for r in range(TOP):
                 partial = work.tile([P, HALF], F32, name="partial", bufs=2 * TOP)

@@ -31,11 +31,15 @@ RUN = 4
 RUNS = H // RUN
 GATHER = 384
 W1_SLOTS = 7
+W2_CODE_SLOTS = 5
 AHEAD = 4
 ORDER = (SHARED,) + tuple(range(E))
-BY_PASS = (ORDER[0], ORDER[-2], ORDER[-1])
-VECTOR_RUNS = 72
+LAST = len(ORDER) - 1
+BY_PASS = ORDER[:1] + ORDER[-3:]
+VECTOR_RUNS = 80
 W2_LOADS = tuple((e, 2) for e in range(0, E - 2, 2)) + ((E - 2, 1), (E - 1, 1), (SHARED, 1))
+SCALAR_PAIRS = tuple(range(0, E - 2, 4))
+Y_BANKS = tuple((e, min(4, E - 1 - e)) for e in range(0, E - 1, 4)) + ((E - 1, 1),)
 SUM_BANKS = 5
 HALF = T // 2
 
@@ -86,7 +90,8 @@ def tile_moe_shr_mlp_gelu_kernel(
                     w1_raw[(e, first + o)] = tile[:, o, :]
 
         def load_w2(first, count):
-            tile = keep.tile([P, count, PACK * N], F32, name="w2_tile_%d" % first)
+            tag = "y_room" if first == SCALAR_PAIRS[-1] else "w2_room_%d" % first
+            tile = keep.tile([P, count, PACK * N], F32, name="w2_tile_%d" % first, tag=tag, align_bytes=64)
             nc.sync.dma_start(out=tile[:], in_=w2[first : first + count].rearrange("g (p j) n -> p g (j n)", j=PACK))
             w2_raw[first] = tile
 
@@ -106,17 +111,17 @@ def tile_moe_shr_mlp_gelu_kernel(
                 nc.scalar.copy(out=dst[:, cut:], in_=src[:, cut:])
             w1_rounded[(e, o)] = tile[:]
 
-        def round_w2(first, count, on_vector):
+        def round_w2(first, count):
             tile = work.tile([P, H * PACK], BF16, name="rounded", align_bytes=64)
             used = tile[:, 0 : count * N * PACK]
             dst = used.rearrange("p (g c i j) -> p g c j i", g=count, i=RUN, j=PACK)
             src = w2_raw[first][:].rearrange("p g (j c i) -> p g c j i", i=RUN, j=PACK)
             if count == 1:
                 dst, src = dst[:, 0], src[:, 0]
-            if on_vector:
-                nc.vector.tensor_copy(out=dst, in_=src)
-            else:
+            if first in SCALAR_PAIRS or first == SHARED:
                 nc.scalar.copy(out=dst, in_=src)
+            else:
+                nc.vector.tensor_copy(out=dst, in_=src)
             w2_rounded[first] = used
 
         def quantise(values, pool, name, bufs):
@@ -160,18 +165,26 @@ def tile_moe_shr_mlp_gelu_kernel(
                     )
                 sums[(e, b)] = bank
 
-        def spent_weights(step):
-            e = ORDER[step]
+        def first_on_scalar(e):
             return w1_raw[(e, 0 if e in BY_PASS else 1)]
+
+        def room_for_pairs(step):
+            if step == LAST:
+                return w2_raw[SCALAR_PAIRS[0]][:].rearrange("p g x -> p (g x)")
+            return first_on_scalar(ORDER[step + 1])
+
+        def room_for_woven(step):
+            if step == LAST:
+                return w2_raw[SCALAR_PAIRS[1]][:].rearrange("p g x -> p (g x)")
+            if ORDER[step + 1] in BY_PASS:
+                return w1_raw[(ORDER[step + 1], 1)]
+            return first_on_scalar(ORDER[step + 2])
 
         def activate(step):
             e = ORDER[step]
-            if step + 1 < len(ORDER):
-                room = spent_weights(step + 1)
-            else:
-                room = keep.tile([P, H // 2], F32, name="last_pairs")[:]
+            room = room_for_pairs(step)
             for b in batches(e):
-                pairs[(e, b)] = room[:, b * H // 2 : (b + 1) * H // 2]
+                pairs[(e, b)] = room[:, b * H + H // 2 : (b + 1) * H]
                 nc.scalar.activation(
                     out=pairs[(e, b)].bitcast(BF16).rearrange("s (u p v) -> s u p v", u=2, v=2),
                     in_=sums[(e, b)][:].rearrange("s (p u v) -> s u p v", u=2, v=2),
@@ -190,10 +203,8 @@ def tile_moe_shr_mlp_gelu_kernel(
         def weave(step):
             e = ORDER[step]
             width = 2 * C * len(batches(e))
-            if step + 2 < len(ORDER):
-                room = spent_weights(step + 2)[:, 2 * H : 2 * H + width]
-            else:
-                room = work.tile([P, width], F32, name="last_woven", bufs=2, align_bytes=64)[:]
+            room = room_for_woven(step)
+            room = room[:, room.shape[1] - width :]
             for first in batches(e)[::2]:
                 count = len(batches(e)[first : first + 2])
                 dst = room[:, 2 * C * first : 2 * C * (first + count)].rearrange("p (b s u) -> p b s u", b=count, u=2)
@@ -204,20 +215,20 @@ def tile_moe_shr_mlp_gelu_kernel(
             e = ORDER[step]
             h_mx[e] = quantise(woven[e].bitcast(BF16), keep, "h_%d" % e, 1)
 
-        y_slots = keep.tile([P, S], F32)
         y_shared = psum.tile([P, T], F32)
+        y_banks = {SHARED: y_shared}
 
-        def second_product(first, count):
+        def second_product(first, count, y_slots):
             words, plane = w2_mx[first]
-            if first == SHARED:
-                bank = y_shared
-            else:
-                bank = psum.tile([P, count * C], F32, name="y_bank", tag="sums", bufs=SUM_BANKS)
+            start, held = [(s, n) for s, n in Y_BANKS + ((SHARED, 1),) if s <= first < s + n][0]
+            if start not in y_banks:
+                y_banks[start] = psum.tile([P, held * C], F32, name="y_bank", tag="sums", bufs=SUM_BANKS)
             for g in range(count):
                 h_words, h_plane = h_mx[first + g]
                 width = h_words.shape[1]
+                place = first - start + g
                 nc.tensor.matmul_mx(
-                    out=bank[:, g * width : (g + 1) * width],
+                    out=y_banks[start][:, place * width : (place + 1) * width],
                     lhsT=words[:, g * N : (g + 1) * N].bitcast(FP8X4),
                     lhsT_scale=plane[:, g * N : (g + 1) * N],
                     rhs=h_words[:].bitcast(FP8X4),
@@ -225,8 +236,8 @@ def tile_moe_shr_mlp_gelu_kernel(
                     start=True,
                     stop=True,
                 )
-            if first != SHARED:
-                nc.scalar.copy(out=y_slots[:, first * C : (first + count) * C], in_=bank[:])
+            if first != SHARED and first + count == start + held:
+                nc.scalar.copy(out=y_slots[:, start * C : (start + held) * C], in_=y_banks[start][:])
 
         gates, token_lists = [], []
 
@@ -252,30 +263,45 @@ def tile_moe_shr_mlp_gelu_kernel(
         for piece in range(S // GATHER):
             gather_slots(piece)
 
-        for step in range(len(ORDER) + 2):
-            if step + AHEAD < len(ORDER):
+        for step, e in enumerate(ORDER):
+            if step + AHEAD <= LAST:
                 load_w1(ORDER[step + AHEAD])
-            elif step + AHEAD == len(ORDER):
+            elif step + AHEAD == LAST + 1:
                 load_rest()
-            if step < len(ORDER):
-                for o in range(PASSES):
-                    round_w1(ORDER[step], o)
-            if step >= 2:
+            for o in range(PASSES):
+                round_w1(e, o)
+            to_quantise = []
+            if step >= 2 and ORDER[step - 2] not in woven:
                 weave(step - 2)
-            if 1 <= step <= len(ORDER):
+                to_quantise.append(step - 2)
+            if step >= 1:
                 activate(step - 1)
                 turn(step - 1)
-            if step < len(ORDER):
-                for o in range(PASSES):
-                    w1_mx[(ORDER[step], o)] = quantise(w1_rounded[(ORDER[step], o)], work, "w1", 4)
-                first_product(ORDER[step])
-            if step >= 2:
-                quantise_hidden(step - 2)
+                if e in BY_PASS:
+                    weave(step - 1)
+                    to_quantise.append(step - 1)
+            for o in range(PASSES):
+                w1_mx[(e, o)] = quantise(w1_rounded[(e, o)], work, "w1", 4)
+            first_product(e)
+            for earlier in to_quantise:
+                quantise_hidden(earlier)
 
-        for turn_number, (first, count) in enumerate(W2_LOADS):
-            round_w2(first, count, turn_number % 2 == 0)
-            w2_mx[first] = quantise(w2_rounded[first], work, "w2", 4)
-            second_product(first, count)
+        y_slots = keep.tile([P, S], F32, tag="y_room", align_bytes=64)
+        waiting = []
+        for first, count in W2_LOADS:
+            round_w2(first, count)
+            if first == SCALAR_PAIRS[0]:
+                activate(LAST)
+                turn(LAST)
+            if first == SCALAR_PAIRS[1]:
+                weave(LAST)
+                quantise_hidden(LAST)
+            w2_mx[first] = quantise(w2_rounded[first], work, "w2", W2_CODE_SLOTS)
+            waiting.append((first, count))
+            if first >= SCALAR_PAIRS[-1]:
+                for load in waiting:
+                    second_product(load[0], load[1], y_slots)
+                waiting = []
 
         for half in range(2):
             cols = slice(half * HALF, (half + 1) * HALF)

from contextlib import ExitStack

import concourse.mybir as mybir
from concourse.masks import make_identity

K, T, E, C, H, N = 1024, 512, 12, 128, 512, 128
TOP = 3
S = E * C
SHARED = E
FLOPS = 2 * (S + T) * (K * H + H * N)

F32 = mybir.dt.float32
BF16 = mybir.dt.bfloat16
I32 = mybir.dt.int32
U32 = mybir.dt.uint32
U16 = mybir.dt.uint16
U8 = mybir.dt.uint8
FP8X4 = mybir.dt.float8_e4m3fn_x4
GELU = mybir.ActivationFunctionType.Gelu_apprx_tanh
MULT = mybir.AluOpType.mult
ADD = mybir.AluOpType.add

P = 128
PACK = 4
K_PASS = P * PACK
PASSES = K // K_PASS
QUADRANT = 32
SCALE_ROWS = 4
PER_COLUMN = 16
RUN = 4
RUNS = H // RUN
GATHER = 384
W1_SLOTS = 7
W2_CODE_SLOTS = 5
AHEAD = 4
ORDER = (SHARED,) + tuple(range(E))
LAST = len(ORDER) - 1
BY_PASS = ORDER[:1] + ORDER[-3:]
VECTOR_RUNS = 80
W2_LOADS = tuple((e, 2) for e in range(0, E - 2, 2)) + ((E - 2, 1), (E - 1, 1), (SHARED, 1))
SCALAR_PAIRS = tuple(range(0, E - 2, 4))
Y_BANKS = tuple((e, min(4, E - 1 - e)) for e in range(0, E - 1, 4)) + ((E - 1, 1),)
SUM_BANKS = 5
HALF = T // 2


def tile_moe_shr_mlp_gelu_kernel(
    tc, x_words, x_scales, w1, w2, gate, offs, pos1, pos2, pos3, out
):
    nc = tc.nc
    with ExitStack() as ctx:
        keep = ctx.enter_context(tc.tile_pool(name="keep", bufs=1))
        ring = ctx.enter_context(tc.tile_pool(name="ring", bufs=W1_SLOTS))
        work = ctx.enter_context(tc.tile_pool(name="work", bufs=4))
        psum = ctx.enter_context(tc.psum_pool(name="psum", bufs=1))

        x_plane = keep.tile([P, T], U8, align_bytes=64)
        nc.vector.memset(x_plane[:].bitcast(I32), 0)
        x_codes = keep.tile([P, PASSES, T], I32, align_bytes=64)
        nc.sync.dma_start(out=x_codes[:], in_=x_words.rearrange("o p t r -> p o (t r)").bitcast(I32))
        slot_list = keep.tile([P, S // PER_COLUMN], U16)
        nc.sync.dma_start(slot_list[:], offs)
        x_rows = keep.tile([P, T // 4], I32)
        for q in range(P // QUADRANT):
            rows = slice(QUADRANT * q, QUADRANT * q + SCALE_ROWS * PASSES)
            blocks = slice(SCALE_ROWS * q, SCALE_ROWS * (q + 1))
            nc.scalar.dma_start(out=x_rows[rows, :], in_=x_scales[:, blocks, :].bitcast(I32))
            nc.vector.tensor_copy(out=x_plane[rows, :].bitcast(I32), in_=x_rows[rows, :])

        warm = keep.tile([P, 2], F32)
        nc.vector.memset(warm[:, 0:1], 0.0)
        nc.scalar.activation(out=warm[:, 1:2], in_=warm[:, 0:1], func=GELU)

        identity = keep.tile([P, P], F32)
        make_identity(nc, identity[:])

        w1_raw, w1_rounded, w1_mx = {}, {}, {}
        w2_raw, w2_rounded, w2_mx = {}, {}, {}
        slot_mx, sums, pairs, turned, woven, h_mx = {}, {}, {}, {}, {}, {}

        def batches(e):
            return range(T // C if e == SHARED else 1)

        def load_w1(e):
            for first, count in ((0, 1), (1, 1)) if e in BY_PASS else ((0, PASSES),):
                tile = ring.tile([P, count, PACK * H], F32, name="w1_tile", align_bytes=64)
                rows = w1[e, first * K_PASS : (first + count) * K_PASS, :]
                nc.sync.dma_start(out=tile[:], in_=rows.rearrange("(o p j) c -> p o (j c)", p=P, j=PACK))
                for o in range(count):
                    w1_raw[(e, first + o)] = tile[:, o, :]

        def load_w2(first, count):
            tag = "y_room" if first == SCALAR_PAIRS[-1] else "w2_room_%d" % first
            tile = keep.tile([P, count, PACK * N], F32, name="w2_tile_%d" % first, tag=tag, align_bytes=64)
            nc.sync.dma_start(out=tile[:], in_=w2[first : first + count].rearrange("g (p j) n -> p g (j n)", j=PACK))
            w2_raw[first] = tile

        def round_w1(e, o):
            tile = work.tile([P, H * PACK], BF16, name="rounded", align_bytes=64)
            dst = tile[:].rearrange("p (c i j) -> p c j i", i=RUN, j=PACK)
            src = w1_raw[(e, o)].rearrange("p (j c i) -> p c j i", i=RUN, j=PACK)
            if e == SHARED:
                cut = 0
            elif e in BY_PASS:
                cut = VECTOR_RUNS
            else:
                cut = RUNS if o == 0 else 0
            if cut > 0:
                nc.vector.tensor_copy(out=dst[:, :cut], in_=src[:, :cut])
            if cut < RUNS:
                nc.scalar.copy(out=dst[:, cut:], in_=src[:, cut:])
            w1_rounded[(e, o)] = tile[:]

        def round_w2(first, count):
            tile = work.tile([P, H * PACK], BF16, name="rounded", align_bytes=64)
            used = tile[:, 0 : count * N * PACK]
            dst = used.rearrange("p (g c i j) -> p g c j i", g=count, i=RUN, j=PACK)
            src = w2_raw[first][:].rearrange("p g (j c i) -> p g c j i", i=RUN, j=PACK)
            if count == 1:
                dst, src = dst[:, 0], src[:, 0]
            if first in SCALAR_PAIRS or first == SHARED:
                nc.scalar.copy(out=dst, in_=src)
            else:
                nc.vector.tensor_copy(out=dst, in_=src)
            w2_rounded[first] = used

        def quantise(values, pool, name, bufs):
            width = values.shape[1] // PACK
            words = pool.tile([P, width], U32, name=name + "_words", bufs=bufs, align_bytes=64)
            plane = pool.tile([P, width], U8, name=name + "_plane", bufs=bufs, align_bytes=64)
            nc.vector.quantize_mx(out=words[:].bitcast(FP8X4), scales=plane[:], in_=values)
            return words, plane

        def gather_slots(piece):
            offsets = slot_list[:, piece * GATHER // PER_COLUMN : (piece + 1) * GATHER // PER_COLUMN]
            words = []
            for o in range(PASSES):
                tile = keep.tile([P, GATHER], U32, name="slot_words_%d_%d" % (piece, o), align_bytes=64)
                nc.vector.tensor_copy(tile[:], x_codes[:, o, :].bitcast(U32).indirect(offsets))
                words.append(tile)
            plane = keep.tile([P, GATHER], U8, name="slot_plane_%d" % piece, align_bytes=64)
            nc.vector.tensor_copy(plane[:], x_plane[:].indirect(offsets))
            slot_mx[piece] = (words, plane)

        def first_product(e):
            for b in batches(e):
                bank = psum.tile([P, H], F32, name="pre_activation", tag="sums", bufs=SUM_BANKS)
                for o in range(PASSES):
                    if e == SHARED:
                        cols = slice(b * C, (b + 1) * C)
                        x_word, x_scale = x_codes[:, o, cols], x_plane[SCALE_ROWS * o : P, cols]
                    else:
                        piece, start = divmod(e * C, GATHER)
                        cols = slice(start, start + C)
                        x_word, x_scale = slot_mx[piece][0][o][:, cols], slot_mx[piece][1][SCALE_ROWS * o : P, cols]
                    words, plane = w1_mx[(e, o)]
                    nc.tensor.matmul_mx(
                        out=bank[:],
                        lhsT=x_word.bitcast(FP8X4),
                        lhsT_scale=x_scale,
                        rhs=words[:].bitcast(FP8X4),
                        rhs_scale=plane[:],
                        start=(o == 0),
                        stop=(o == PASSES - 1),
                    )
                sums[(e, b)] = bank

        def first_on_scalar(e):
            return w1_raw[(e, 0 if e in BY_PASS else 1)]

        def room_for_pairs(step):
            if step == LAST:
                return w2_raw[SCALAR_PAIRS[0]][:].rearrange("p g x -> p (g x)")
            return first_on_scalar(ORDER[step + 1])

        def room_for_woven(step):
            if step == LAST:
                return w2_raw[SCALAR_PAIRS[1]][:].rearrange("p g x -> p (g x)")
            if ORDER[step + 1] in BY_PASS:
                return w1_raw[(ORDER[step + 1], 1)]
            return first_on_scalar(ORDER[step + 2])

        def activate(step):
            e = ORDER[step]
            room = room_for_pairs(step)
            for b in batches(e):
                pairs[(e, b)] = room[:, b * H + H // 2 : (b + 1) * H]
                nc.scalar.activation(
                    out=pairs[(e, b)].bitcast(BF16).rearrange("s (u p v) -> s u p v", u=2, v=2),
                    in_=sums[(e, b)][:].rearrange("s (p u v) -> s u p v", u=2, v=2),
                    func=GELU,
                )

        def turn(step):
            e = ORDER[step]
            for first in batches(e)[::2]:
                bank = psum.tile([P, 2, 2, C], F32, name="turned_pairs", bufs=2)
                for b in batches(e)[first : first + 2]:
                    for u in range(2):
                        nc.tensor.transpose(bank[:, b - first, u, :], pairs[(e, b)][:, u * P : (u + 1) * P], identity[:])
                turned[(e, first)] = bank

        def weave(step):
            e = ORDER[step]
            width = 2 * C * len(batches(e))
            room = room_for_woven(step)
            room = room[:, room.shape[1] - width :]
            for first in batches(e)[::2]:
                count = len(batches(e)[first : first + 2])
                dst = room[:, 2 * C * first : 2 * C * (first + count)].rearrange("p (b s u) -> p b s u", b=count, u=2)
                nc.scalar.copy(out=dst, in_=turned[(e, first)][:, 0:count].rearrange("p b u s -> p b s u"))
            woven[e] = room

        def quantise_hidden(step):
            e = ORDER[step]
            h_mx[e] = quantise(woven[e].bitcast(BF16), keep, "h_%d" % e, 1)

        y_shared = psum.tile([P, T], F32)
        y_banks = {SHARED: y_shared}

        def second_product(first, count, y_slots):
            words, plane = w2_mx[first]
            start, held = [(s, n) for s, n in Y_BANKS + ((SHARED, 1),) if s <= first < s + n][0]
            if start not in y_banks:
                y_banks[start] = psum.tile([P, held * C], F32, name="y_bank", tag="sums", bufs=SUM_BANKS)
            for g in range(count):
                h_words, h_plane = h_mx[first + g]
                width = h_words.shape[1]
                place = first - start + g
                nc.tensor.matmul_mx(
                    out=y_banks[start][:, place * width : (place + 1) * width],
                    lhsT=words[:, g * N : (g + 1) * N].bitcast(FP8X4),
                    lhsT_scale=plane[:, g * N : (g + 1) * N],
                    rhs=h_words[:].bitcast(FP8X4),
                    rhs_scale=h_plane[:],
                    start=True,
                    stop=True,
                )
            if first != SHARED and first + count == start + held:
                nc.scalar.copy(out=y_slots[:, start * C : (start + held) * C], in_=y_banks[start][:])

        gates, token_lists = [], []

        def load_gate(r):
            tile = keep.tile([P, T], F32, name="gate_%d" % r)
            nc.sync.dma_start(out=tile[:], in_=gate[r])
            gates.append(tile)

        def load_rest():
            for first, count in W2_LOADS[:-1]:
                load_w2(first, count)
            load_gate(0)
            for r, pos in enumerate((pos1, pos2, pos3)):
                tile = keep.tile([P, T // PER_COLUMN], U16, name="token_list_%d" % r)
                nc.sync.dma_start(tile[:], pos)
                token_lists.append(tile)
            load_w2(*W2_LOADS[-1])
            for r in range(1, TOP):
                load_gate(r)

        for e in ORDER[:AHEAD]:
            load_w1(e)
        for piece in range(S // GATHER):
            gather_slots(piece)

        for step, e in enumerate(ORDER):
            if step + AHEAD <= LAST:
                load_w1(ORDER[step + AHEAD])
            elif step + AHEAD == LAST + 1:
                load_rest()
            for o in range(PASSES):
                round_w1(e, o)
            to_quantise = []
            if step >= 2 and ORDER[step - 2] not in woven:
                weave(step - 2)
                to_quantise.append(step - 2)
            if step >= 1:
                activate(step - 1)
                turn(step - 1)
                if e in BY_PASS:
                    weave(step - 1)
                    to_quantise.append(step - 1)
            for o in range(PASSES):
                w1_mx[(e, o)] = quantise(w1_rounded[(e, o)], work, "w1", 4)
            first_product(e)
            for earlier in to_quantise:
                quantise_hidden(earlier)

        y_slots = keep.tile([P, S], F32, tag="y_room", align_bytes=64)
        waiting = []
        for first, count in W2_LOADS:
            round_w2(first, count)
            if first == SCALAR_PAIRS[0]:
                activate(LAST)
                turn(LAST)
            if first == SCALAR_PAIRS[1]:
                weave(LAST)
                quantise_hidden(LAST)
            w2_mx[first] = quantise(w2_rounded[first], work, "w2", W2_CODE_SLOTS)
            waiting.append((first, count))
            if first >= SCALAR_PAIRS[-1]:
                for load in waiting:
                    second_product(load[0], load[1], y_slots)
                waiting = []

        for half in range(2):
            cols = slice(half * HALF, (half + 1) * HALF)
            total = y_shared[:, cols]
            terms = []
            for r in range(TOP):
                term = work.tile([P, HALF], F32, name="term", bufs=2 * TOP)
                offsets = token_lists[r][:, half * HALF // PER_COLUMN : (half + 1) * HALF // PER_COLUMN]
                nc.vector.tensor_tensor(term[:], y_slots[:].indirect(offsets), gates[r][:, cols], MULT)
                terms.append(term)
            for r in range(TOP):
                partial = work.tile([P, HALF], F32, name="partial", bufs=2 * TOP)
                nc.vector.tensor_tensor(partial[:], terms[r][:], total, ADD)
                total = partial[:]
            nc.sync.dma_start(out=out[:, cols], in_=total)
